import numpy as np, ml_dtypes
CORES = [10,18,34,42,58,66,82,90,98,106]
N = 10
import mx_ref
NC, G = 128, 4
C = np.float32(0.023)
CNT = [[0,20,16,8,44,12,20,0,0,8],[0,0,0,12,8,16,0,48,32,12],[0,0,0,20,32,0,4,16,48,8],[24,4,0,0,24,36,24,4,0,12],[16,32,0,32,0,4,0,20,0,24],[0,16,4,12,0,0,32,28,24,12],[0,12,8,12,4,44,0,0,12,36],[52,4,28,16,12,16,0,0,0,0],[20,28,24,16,4,0,20,0,0,16],[16,12,48,0,0,0,28,12,12,0]]
OFF = [[sum(c[:e]) for e in range(N + 1)] for c in CNT]
BF = ml_dtypes.bfloat16
def cut(t, i, w=512):
    return t[:, w * i:w * i + w]
def tile(rs):
    return np.stack(rs, axis=2).reshape(128, -1).astype(BF)
def layer(w, X):
    out = []
    for i in range(G):
        for t in range(len(X)):
            p = mx_ref.matmul(mx_ref.quantize(cut(w, len(X) * i + t)), X[t])
            z = p if t == 0 else z + p
        out.append(z)
    return out
def act(Z):
    return [np.maximum(z, 0) * C for z in Z]
def setup_inputs(rng):
    def f(*shape):
        return mx_ref.flush((rng.standard_normal(shape, dtype=np.float32) * np.exp2(rng.integers(-2, 3, shape[:-1] + (1,)))).astype(BF))
    return {"x": f(N, 128, 4 * NC), "w1": f(N, 128, G * 512), "w2": f(N, 128, 512), "s1": f(N, 128, G * 512), "s2": f(N, 128, 512)}
def setup_inputs_blocks(rng):
    d = setup_inputs(rng)
    for k in ("x", "w1", "w2", "s1", "s2"): d[k] = mx_ref.spread(d[k], rng, 4)
    return d
def setup_inputs_wide(rng):
    d = setup_inputs(rng)
    for k in ("x", "w1", "w2", "s1", "s2"): d[k] = mx_ref.flush((d[k].astype(np.float32) * np.exp2(rng.integers(-8, 9, (N, 1, 1))).astype(np.float32)).astype(BF))
    return d
def setup_inputs_zeros(rng):
    d = setup_inputs(rng); v = d["x"].reshape(N, 128, -1, 4).copy()
    v[np.broadcast_to((rng.random((N, 1, v.shape[2], 1)) < 0.33), v.shape)] = 0
    d["x"] = v.reshape(d["x"].shape)
    return d
def reference(x, w1, w2, s1, s2):
    y = np.zeros((N, 128, NC), np.float32)
    for j in range(N):
        y[j] = mx_ref.matmul(mx_ref.quantize(s2[j]), mx_ref.quantize(tile(act(layer(s1[j], [mx_ref.quantize(x[j])])))))
    for e in range(N):
        t = np.concatenate([x[j][:, 4 * OFF[j][e]:4 * OFF[j][e + 1]] for j in range(N)], axis=1)
        p = mx_ref.matmul(mx_ref.quantize(w2[e]), mx_ref.quantize(tile(act(layer(w1[e], [mx_ref.quantize(t)])))))
        c = 0
        for j in range(N):
            a, b = OFF[j][e], OFF[j][e + 1]
            y[j][:, a:b] = y[j][:, a:b] + p[:, c:c + b - a]; c += b - a
    return {"y": y}

@@ -1,0 +1,176 @@
+from concourse.bass import DstId, RemoteDMATransfer
+from concourse.mybir import dt, AluOpType, ActivationFunctionType
+
+N, NC, G, C = 10, 128, 4, 0.023
+CAP = 320
+
+SCRATCH = {
+    "xb": ("sbuf", [128, 4 * NC], "bfloat16"),
+    "w1b": ("sbuf", [128, G * 512], "bfloat16"),
+    "w2b": ("sbuf", [128, 512], "bfloat16"),
+    "s1b": ("sbuf", [128, G * 512], "bfloat16"),
+    "s2b": ("sbuf", [128, 512], "bfloat16"),
+    "xq": ("sbuf", [128, NC], "float8_e4m3fn_x4"), "xs": ("sbuf", [128, NC], "uint8"),
+    "w1q": ("sbuf", [128, G * 128], "float8_e4m3fn_x4"), "w1s": ("sbuf", [128, G * 128], "uint8"),
+    "w2q": ("sbuf", [128, 128], "float8_e4m3fn_x4"), "w2s": ("sbuf", [128, 128], "uint8"),
+    "s1q": ("sbuf", [128, G * 128], "float8_e4m3fn_x4"), "s1s": ("sbuf", [128, G * 128], "uint8"),
+    "s2q": ("sbuf", [128, 128], "float8_e4m3fn_x4"), "s2s": ("sbuf", [128, 128], "uint8"),
+    "bq": ("sbuf", [128, CAP], "float8_e4m3fn_x4"), "bs": ("sbuf", [128, CAP], "uint8"),
+    "hb": ("sbuf", [128, 4 * CAP], "bfloat16"),
+    "hq": ("sbuf", [128, CAP], "float8_e4m3fn_x4"), "hs": ("sbuf", [128, CAP], "uint8"),
+    "kb": ("sbuf", [128, 4 * NC], "bfloat16"),
+    "kq": ("sbuf", [128, NC], "float8_e4m3fn_x4"), "ks": ("sbuf", [128, NC], "uint8"),
+    "pb": ("sbuf", [128, CAP], "float32"),
+    "land": ("sbuf", [128, NC], "float32"),
+    "yb": ("sbuf", [128, NC], "float32"),
+    "zp": ("psum", [128, 512 * G], "float32"),
+    "pp": ("psum", [128, 512], "float32"),
+    "up": ("psum", [128, 512], "float32"),
+}
+SEMAPHORES = ["ldx", "ldw", "lds", "xdone", "wdone", "sdone", "sent", "xin", "z0", "z1", "z2", "z3", "hact", "hdone", "pmm",
+              "pcopy", "y0", "y1", "y2", "y3", "kact", "kdone", "umm", "back", "returned", "ydone", "stored"]
+
+
+def _plan(cnt, engines):
+    win, slot, ncol = [], [{} for _ in range(N)], [0] * N
+    for j in range(N):
+        w = 4
+        while sum(-(-c // w) for c in cnt[j]) > engines:
+            w += 4
+        pieces, a = [], 0
+        for e in range(N):
+            c = cnt[j][e]
+            if c:
+                k = -(-c // w)
+                s = min(a, NC - k * w)
+                for i in range(k):
+                    pieces.append((e, s + i * w, ncol[e] + i * w))
+                slot[e][j] = ncol[e] + a - s
+                ncol[e] += k * w
+            a += c
+        win.append((w, pieces))
+    return win, slot, ncol
+
+
+def _returns(runs):
+    by = {}
+    for w, j in runs:
+        by.setdefault(w, []).append(j)
+    out = []
+    for w in sorted(by):
+        js = by[w]
+        while js:
+            k = 1
+            while 2 * k <= min(len(js), 8):
+                k *= 2
+            out.append((w, js[:k]))
+            js = js[k:]
+    out.sort(key=lambda g: (-len(g[1]), -g[0]))
+    return out
+
+
+def rank_program(g, core, T, topo):
+    rank = T.rank_of(core)
+    if rank is None:
+        return
+    cnt, cores = T.tables["CNT"], T.cores
+    relu = ActivationFunctionType.Relu
+    mx, mul, add = AluOpType.max, AluOpType.mult, AluOpType.add
+    S = T.sem
+
+    def engines(dst):
+        m = topo.mask(core, dst)
+        return [1 << b for b in range(m.bit_length()) if m >> b & 1]
+
+    def transfer(dst, first, n, sem, src, out):
+        rid, pid, _ = topo.addr(dst)
+        return RemoteDMATransfer(dst_ids=[DstId(rid=rid, pnc=pid)], dma_engine_mask=sum(engines(dst)[first:first + n]),
+                                 remote_sem=sem, src=src, dst=out)
+
+    ne = min(len(engines(c)) for c in cores if c != core)
+    win, slot, ncol = _plan(cnt, ne)
+    n = ncol[rank]
+    width, pieces = win[rank]
+    off = [[sum(r[:e]) for e in range(N)] for r in cnt]
+
+    g.sync.dma_start(T.xb[:], T.x[:]).then_inc(S.ldx, 16)
+    g.sync.dma_start(T.w1b[:], T.w1[:]).then_inc(S.ldw, 16)
+    g.sync.dma_start(T.w2b[:], T.w2[:]).then_inc(S.ldw, 16)
+    g.sync.wait_ge(S.sent, 2 * len(pieces))
+    g.sync.dma_start(T.s1b[:], T.s1[:]).then_inc(S.lds, 16)
+    g.sync.dma_start(T.s2b[:], T.s2[:]).then_inc(S.lds, 16)
+    g.sync.wait_ge(S.ydone, 1)
+    g.sync.dma_start(T.y[:], T.yb[:]).then_inc(S.stored, 16)
+    g.sync.wait_ge(S.stored, 16)
+
+    v = g.vector
+    v.wait_ge(S.ldx, 16)
+    v.quantize_mx(T.xq[:], T.xs[:], T.xb[:]).then_inc(S.xdone, 1)
+    v.wait_ge(S.ldw, 32)
+    for i in range(G):
+        v.quantize_mx(T.w1q[:, 128 * i:128 * i + 128], T.w1s[:, 128 * i:128 * i + 128],
+                      T.w1b[:, 512 * i:512 * i + 512]).then_inc(S.wdone, 1)
+    v.quantize_mx(T.w2q[:], T.w2s[:], T.w2b[:]).then_inc(S.wdone, 1)
+
+    g.wait_ge(S.xdone, 1)
+    g.remote_dma_fused([transfer(cores[e], k, 1, S.xin, T.xq[:, a:a + width].bitcast(dt.uint8),
+                                 T.bq[:, b:b + width].bitcast(dt.uint8)) for k, (e, a, b) in enumerate(pieces)],
+                       local_sem=S.sent)
+    g.remote_dma_fused([transfer(cores[e], k, 1, S.xin, T.xs[:, a:a + width], T.bs[:, b:b + width])
+                        for k, (e, a, b) in enumerate(pieces)], local_sem=S.sent)
+
+    def hidden(wq, ws, rq, rs, m, zsem, tile, act):
+        for b in range(G):
+            g.tensor.matmul_mx(T.zp[:, 512 * b:512 * b + m], wq[:, 128 * b:128 * b + 128], ws[:, 128 * b:128 * b + 128],
+                               rq[:, 0:m], rs[:, 0:m], True, True).then_inc(S[zsem + str(b)], 1)
+        for b in (0, 2):
+            g.scalar.wait_ge(S[zsem + str(b)], 1)
+            g.scalar.activation(tile[:, b:4 * m:4], T.zp[:, 512 * b:512 * b + m], relu, scale=C).then_inc(act, 1)
+        for b in (1, 3):
+            v.wait_ge(S[zsem + str(b)], 1)
+            v.tensor_scalar(tile[:, b:4 * m:4], T.zp[:, 512 * b:512 * b + m], 0.0, C, mx, mul).then_inc(act, 1)
+        v.wait_ge(act, 4)
+
+    arrivals = sum(2 for j in range(N) for p in win[j][1] if p[0] == rank)
+    g.tensor.wait_ge(S.wdone, G + 1)
+    g.tensor.wait_ge(S.xin, arrivals)
+    hidden(T.w1q, T.w1s, T.bq, T.bs, n, "z", T.hb, S.hact)
+    v.quantize_mx(T.hq[:, 0:n], T.hs[:, 0:n], T.hb[:, 0:4 * n]).then_inc(S.hdone, 1)
+    g.tensor.wait_ge(S.hdone, 1)
+    g.tensor.matmul_mx(T.pp[:, 0:n], T.w2q[:], T.w2s[:], T.hq[:, 0:n], T.hs[:, 0:n], True, True).then_inc(S.pmm, 1)
+    v.wait_ge(S.pmm, 1)
+    v.tensor_copy(T.pb[:, 0:n], T.pp[:, 0:n]).then_inc(S.pcopy, 1)
+
+    g.wait_ge(S.pcopy, 1)
+    left = 0
+    for w, js in _returns([(cnt[j][rank], j) for j in range(N) if cnt[j][rank]]):
+        k = ne // len(js)
+        while ne % k or k & (k - 1):
+            k -= 1
+        g.remote_dma_fused([transfer(cores[j], k * i, k, S.back, T.pb[:, slot[rank][j]:slot[rank][j] + w],
+                                     T.land[:, off[j][rank]:off[j][rank] + w]) for i, j in enumerate(js)],
+                           local_sem=S.returned)
+        left += k * len(js)
+    g.wait_ge(S.returned, left)
+
+    v.wait_ge(S.lds, 32)
+    for i in range(G):
+        v.quantize_mx(T.s1q[:, 128 * i:128 * i + 128], T.s1s[:, 128 * i:128 * i + 128],
+                      T.s1b[:, 512 * i:512 * i + 512]).then_inc(S.sdone, 1)
+    v.quantize_mx(T.s2q[:], T.s2s[:], T.s2b[:]).then_inc(S.sdone, 1)
+    g.tensor.wait_ge(S.xdone, 1)
+    g.tensor.wait_ge(S.sdone, G + 1)
+    hidden(T.s1q, T.s1s, T.xq, T.xs, NC, "y", T.kb, S.kact)
+    v.quantize_mx(T.kq[:], T.ks[:], T.kb[:]).then_inc(S.kdone, 1)
+    g.tensor.wait_ge(S.kdone, 1)
+    g.tensor.matmul_mx(T.up[:, 0:NC], T.s2q[:], T.s2s[:], T.kq[:], T.ks[:], True, True).then_inc(S.umm, 1)
+
+    inc = 0
+    for e in range(N):
+        if cnt[rank][e]:
+            for w, js in _returns([(cnt[j][e], j) for j in range(N) if cnt[j][e]]):
+                if rank in js:
+                    inc += ne // len(js)
+    v.wait_ge(S.umm, 1)
+    v.wait_ge(S.back, inc)
+    v.tensor_tensor(T.yb[:], T.up[:, 0:NC], T.land[:], add).then_inc(S.ydone, 1)

@@ -2,7 +2,20 @@ from concourse.bass import DstId, RemoteDMATransfer
 from concourse.mybir import dt, AluOpType, ActivationFunctionType
 
 N, NC, G, C = 10, 128, 4, 0.023
-CAP = 320
+CAP = 192
+
+WIDTHS = [
+    [24, 24, 12, 24, 12, 24, 12],
+    [12, 12, 24, 24, 24, 12],
+    [24, 16, 16, 16, 24, 16],
+    [24, 12, 24, 24, 24, 12, 12],
+    [12, 32, 32, 12, 32, 12],
+    [16, 16, 16, 16, 28, 28, 16],
+    [12, 12, 12, 12, 44, 12, 44],
+    [28, 16, 28, 16, 16, 16],
+    [28, 28, 28, 28, 8, 28, 8],
+    [16, 16, 16, 28, 16, 16],
+]
 
 SCRATCH = {
     "xb": ("sbuf", [128, 4 * NC], "bfloat16"),
@@ -31,24 +44,26 @@ SEMAPHORES = ["ldx", "ldw", "lds", "xdone", "wdone", "sdone", "sent", "xin", "z0
               "pcopy", "y0", "y1", "y2", "y3", "kact", "kdone", "umm", "back", "returned", "ydone", "stored"]
 
 
-def _plan(cnt, engines):
+def _plan(cnt):
     win, slot, ncol = [], [{} for _ in range(N)], [0] * N
     for j in range(N):
-        w = 4
-        while sum(-(-c // w) for c in cnt[j]) > engines:
-            w += 4
-        pieces, a = [], 0
+        by, a, widths = {}, 0, list(WIDTHS[j])
         for e in range(N):
             c = cnt[j][e]
             if c:
+                w = widths.pop(0)
                 k = -(-c // w)
                 s = min(a, NC - k * w)
                 for i in range(k):
-                    pieces.append((e, s + i * w, ncol[e] + i * w))
+                    by.setdefault(w, []).append((e, s + i * w, ncol[e] + i * w))
                 slot[e][j] = ncol[e] + a - s
                 ncol[e] += k * w
             a += c
-        win.append((w, pieces))
+        calls, eng = [], 0
+        for w in sorted(by, reverse=True):
+            calls.append((w, [p + (eng + i,) for i, p in enumerate(by[w])]))
+            eng += len(by[w])
+        win.append(calls)
     return win, slot, ncol
 
 
@@ -88,15 +103,15 @@ def rank_program(g, core, T, topo):
                                  remote_sem=sem, src=src, dst=out)
 
     ne = min(len(engines(c)) for c in cores if c != core)
-    win, slot, ncol = _plan(cnt, ne)
+    win, slot, ncol = _plan(cnt)
     n = ncol[rank]
-    width, pieces = win[rank]
+    windows = sum(len(p) for _, p in win[rank])
     off = [[sum(r[:e]) for e in range(N)] for r in cnt]
 
     g.sync.dma_start(T.xb[:], T.x[:]).then_inc(S.ldx, 16)
     g.sync.dma_start(T.w1b[:], T.w1[:]).then_inc(S.ldw, 16)
     g.sync.dma_start(T.w2b[:], T.w2[:]).then_inc(S.ldw, 16)
-    g.sync.wait_ge(S.sent, 2 * len(pieces))
+    g.sync.wait_ge(S.sent, 2 * windows)
     g.sync.dma_start(T.s1b[:], T.s1[:]).then_inc(S.lds, 16)
     g.sync.dma_start(T.s2b[:], T.s2[:]).then_inc(S.lds, 16)
     g.sync.wait_ge(S.ydone, 1)
@@ -113,11 +128,12 @@ def rank_program(g, core, T, topo):
     v.quantize_mx(T.w2q[:], T.w2s[:], T.w2b[:]).then_inc(S.wdone, 1)
 
     g.wait_ge(S.xdone, 1)
-    g.remote_dma_fused([transfer(cores[e], k, 1, S.xin, T.xq[:, a:a + width].bitcast(dt.uint8),
-                                 T.bq[:, b:b + width].bitcast(dt.uint8)) for k, (e, a, b) in enumerate(pieces)],
-                       local_sem=S.sent)
-    g.remote_dma_fused([transfer(cores[e], k, 1, S.xin, T.xs[:, a:a + width], T.bs[:, b:b + width])
-                        for k, (e, a, b) in enumerate(pieces)], local_sem=S.sent)
+    for width, pieces in win[rank]:
+        g.remote_dma_fused([transfer(cores[e], k, 1, S.xin, T.xq[:, a:a + width].bitcast(dt.uint8),
+                                     T.bq[:, b:b + width].bitcast(dt.uint8)) for e, a, b, k in pieces], local_sem=S.sent)
+    for width, pieces in win[rank]:
+        g.remote_dma_fused([transfer(cores[e], k, 1, S.xin, T.xs[:, a:a + width], T.bs[:, b:b + width])
+                            for e, a, b, k in pieces], local_sem=S.sent)
 
     def hidden(wq, ws, rq, rs, m, zsem, tile, act):
         for b in range(G):
@@ -131,7 +147,7 @@ def rank_program(g, core, T, topo):
             v.tensor_scalar(tile[:, b:4 * m:4], T.zp[:, 512 * b:512 * b + m], 0.0, C, mx, mul).then_inc(act, 1)
         v.wait_ge(act, 4)
 
-    arrivals = sum(2 for j in range(N) for p in win[j][1] if p[0] == rank)
+    arrivals = sum(2 for j in range(N) for _, ps in win[j] for p in ps if p[0] == rank)
     g.tensor.wait_ge(S.wdone, G + 1)
     g.tensor.wait_ge(S.xin, arrivals)
     hidden(T.w1q, T.w1s, T.bq, T.bs, n, "z", T.hb, S.hact)
@@ -145,8 +161,6 @@ def rank_program(g, core, T, topo):
     left = 0
     for w, js in _returns([(cnt[j][rank], j) for j in range(N) if cnt[j][rank]]):
         k = ne // len(js)
-        while ne % k or k & (k - 1):
-            k -= 1
         g.remote_dma_fused([transfer(cores[j], k * i, k, S.back, T.pb[:, slot[rank][j]:slot[rank][j] + w],
                                      T.land[:, off[j][rank]:off[j][rank] + w]) for i, j in enumerate(js)],
                            local_sem=S.returned)

@@ -2,20 +2,13 @@ from concourse.bass import DstId, RemoteDMATransfer
 from concourse.mybir import dt, AluOpType, ActivationFunctionType
 
 N, NC, G, C = 10, 128, 4, 0.023
-CAP = 192
 
-WIDTHS = [
-    [24, 24, 12, 24, 12, 24, 12],
-    [12, 12, 24, 24, 24, 12],
-    [24, 16, 16, 16, 24, 16],
-    [24, 12, 24, 24, 24, 12, 12],
-    [12, 32, 32, 12, 32, 12],
-    [16, 16, 16, 16, 28, 28, 16],
-    [12, 12, 12, 12, 44, 12, 44],
-    [28, 16, 28, 16, 16, 16],
-    [28, 28, 28, 28, 8, 28, 8],
-    [16, 16, 16, 28, 16, 16],
-]
+SEND = [(2, [1, 9, 3, 4, 5, 2, 6]), (2, [3, 4, 5, 7, 8, 9]), (2, [8, 4, 9, 3, 6, 7]), (2, [9, 7, 1, 6, 5, 4, 0]),
+        (4, [9, 5, 7, 0, 3, 1]), (2, [3, 6, 7, 8, 1, 9, 2]), (2, [8, 3, 4, 2, 1, 9, 5]), (4, [3, 2, 1, 5, 0, 4]),
+        (2, [9, 1, 0, 2, 3, 4, 6]), (2, [0, 7, 6, 8, 2, 1])]
+BACK = [(2, [7, 3, 9, 4, 8]), (2, [3, 8, 5, 0, 4, 7, 9, 6]), (2, [8, 9, 7, 0, 5, 6]), (2, [4, 6, 2, 7, 0, 5, 1, 8]),
+        (2, [0, 2, 3, 7, 8, 1, 6]), (2, [6, 3, 0, 7, 1, 4]), (2, [2, 0, 5, 9, 3, 8]), (2, [5, 1, 4, 2, 9, 3]),
+        (4, [2, 1, 6, 5, 9]), (2, [6, 4, 1, 8, 0, 2, 5, 3])]
 
 SCRATCH = {
     "xb": ("sbuf", [128, 4 * NC], "bfloat16"),
@@ -28,60 +21,40 @@ SCRATCH = {
     "w2q": ("sbuf", [128, 128], "float8_e4m3fn_x4"), "w2s": ("sbuf", [128, 128], "uint8"),
     "s1q": ("sbuf", [128, G * 128], "float8_e4m3fn_x4"), "s1s": ("sbuf", [128, G * 128], "uint8"),
     "s2q": ("sbuf", [128, 128], "float8_e4m3fn_x4"), "s2s": ("sbuf", [128, 128], "uint8"),
-    "bq": ("sbuf", [128, CAP], "float8_e4m3fn_x4"), "bs": ("sbuf", [128, CAP], "uint8"),
-    "hb": ("sbuf", [128, 4 * CAP], "bfloat16"),
-    "hq": ("sbuf", [128, CAP], "float8_e4m3fn_x4"), "hs": ("sbuf", [128, CAP], "uint8"),
+    "bq": ("sbuf", [128, NC], "float8_e4m3fn_x4"), "bs": ("sbuf", [128, NC], "uint8"),
+    "hb": ("sbuf", [128, 4 * NC], "bfloat16"),
+    "hq": ("sbuf", [128, NC], "float8_e4m3fn_x4"), "hs": ("sbuf", [128, NC], "uint8"),
     "kb": ("sbuf", [128, 4 * NC], "bfloat16"),
     "kq": ("sbuf", [128, NC], "float8_e4m3fn_x4"), "ks": ("sbuf", [128, NC], "uint8"),
-    "pb": ("sbuf", [128, CAP], "float32"),
+    "pb": ("sbuf", [128, NC], "float32"),
     "land": ("sbuf", [128, NC], "float32"),
     "yb": ("sbuf", [128, NC], "float32"),
     "zp": ("psum", [128, 512 * G], "float32"),
     "pp": ("psum", [128, 512], "float32"),
     "up": ("psum", [128, 512], "float32"),
 }
-SEMAPHORES = ["ldx", "ldw", "lds", "xdone", "wdone", "sdone", "sent", "xin", "z0", "z1", "z2", "z3", "hact", "hdone", "pmm",
-              "pcopy", "y0", "y1", "y2", "y3", "kact", "kdone", "umm", "back", "returned", "ydone", "stored"]
+SEMAPHORES = ["ldx", "ldw", "lds1", "lds2", "xdone", "wdone", "sent1", "sent2", "xin", "z0", "z1", "z2", "z3", "hact", "hdone",
+              "pmm", "pcopy1", "pcopy2", "s0", "s1", "s2", "s3", "s4", "y0", "y1", "y2", "y3", "kact", "kdone", "umm", "back",
+              "returned", "ydone", "stored"]
 
 
-def _plan(cnt):
-    win, slot, ncol = [], [{} for _ in range(N)], [0] * N
-    for j in range(N):
-        by, a, widths = {}, 0, list(WIDTHS[j])
-        for e in range(N):
-            c = cnt[j][e]
-            if c:
-                w = widths.pop(0)
-                k = -(-c // w)
-                s = min(a, NC - k * w)
-                for i in range(k):
-                    by.setdefault(w, []).append((e, s + i * w, ncol[e] + i * w))
-                slot[e][j] = ncol[e] + a - s
-                ncol[e] += k * w
-            a += c
-        calls, eng = [], 0
-        for w in sorted(by, reverse=True):
-            calls.append((w, [p + (eng + i,) for i, p in enumerate(by[w])]))
-            eng += len(by[w])
-        win.append(calls)
-    return win, slot, ncol
-
-
-def _returns(runs):
-    by = {}
-    for w, j in runs:
-        by.setdefault(w, []).append(j)
+def _steps(plan, width, engines):
+    lanes, order = plan
     out = []
-    for w in sorted(by):
-        js = by[w]
-        while js:
-            k = 1
-            while 2 * k <= min(len(js), 8):
-                k *= 2
-            out.append((w, js[:k]))
-            js = js[k:]
-    out.sort(key=lambda g: (-len(g[1]), -g[0]))
+    for s in range(0, len(order), lanes):
+        js = order[s:s + lanes]
+        k = engines // lanes
+        while 2 * k * len(js) <= engines:
+            k *= 2
+        by = {}
+        for i, j in enumerate(js):
+            by.setdefault(width[j], []).append((j, k * i, k))
+        out.append(list(by.items()))
     return out
+
+
+def _engines_of(steps, rank):
+    return sum(k for step in steps for _, ds in step for j, _, k in ds if j == rank)
 
 
 def rank_program(g, core, T, topo):
@@ -91,34 +64,34 @@ def rank_program(g, core, T, topo):
     cnt, cores = T.tables["CNT"], T.cores
     relu = ActivationFunctionType.Relu
     mx, mul, add = AluOpType.max, AluOpType.mult, AluOpType.add
-    S = T.sem
+    S, v = T.sem, g.vector
+
+    off = [[sum(r[:e]) for e in range(N)] for r in cnt]
+    slot = [{} for _ in range(N)]
+    for e in range(N):
+        a = 0
+        for j in BACK[e][1]:
+            slot[e][j] = a
+            a += cnt[j][e]
 
     def engines(dst):
         m = topo.mask(core, dst)
-        return [1 << b for b in range(m.bit_length()) if m >> b & 1]
-
-    def transfer(dst, first, n, sem, src, out):
-        rid, pid, _ = topo.addr(dst)
-        return RemoteDMATransfer(dst_ids=[DstId(rid=rid, pnc=pid)], dma_engine_mask=sum(engines(dst)[first:first + n]),
-                                 remote_sem=sem, src=src, dst=out)
+        return [1 << i for i in range(m.bit_length()) if m >> i & 1]
 
     ne = min(len(engines(c)) for c in cores if c != core)
-    win, slot, ncol = _plan(cnt)
-    n = ncol[rank]
-    windows = sum(len(p) for _, p in win[rank])
-    off = [[sum(r[:e]) for e in range(N)] for r in cnt]
+    outward = [_steps(SEND[j], cnt[j], ne) for j in range(N)]
+    homeward = [_steps(BACK[e], [r[e] for r in cnt], ne) for e in range(N)]
 
-    g.sync.dma_start(T.xb[:], T.x[:]).then_inc(S.ldx, 16)
-    g.sync.dma_start(T.w1b[:], T.w1[:]).then_inc(S.ldw, 16)
-    g.sync.dma_start(T.w2b[:], T.w2[:]).then_inc(S.ldw, 16)
-    g.sync.wait_ge(S.sent, 2 * windows)
-    g.sync.dma_start(T.s1b[:], T.s1[:]).then_inc(S.lds, 16)
-    g.sync.dma_start(T.s2b[:], T.s2[:]).then_inc(S.lds, 16)
-    g.sync.wait_ge(S.ydone, 1)
-    g.sync.dma_start(T.y[:], T.yb[:]).then_inc(S.stored, 16)
-    g.sync.wait_ge(S.stored, 16)
+    def send(ds, sem, local, piece):
+        ts = []
+        for j, first, k in ds:
+            rid, pid, _ = topo.addr(cores[j])
+            src, dst = piece(j)
+            ts.append(RemoteDMATransfer(dst_ids=[DstId(rid=rid, pnc=pid)], remote_sem=sem, src=src, dst=dst,
+                                        dma_engine_mask=sum(engines(cores[j])[first:first + k])))
+        g.remote_dma_fused(ts, local_sem=local)
+        return sum(k for _, _, k in ds)
 
-    v = g.vector
     v.wait_ge(S.ldx, 16)
     v.quantize_mx(T.xq[:], T.xs[:], T.xb[:]).then_inc(S.xdone, 1)
     v.wait_ge(S.ldw, 32)
@@ -128,63 +101,76 @@ def rank_program(g, core, T, topo):
     v.quantize_mx(T.w2q[:], T.w2s[:], T.w2b[:]).then_inc(S.wdone, 1)
 
     g.wait_ge(S.xdone, 1)
-    for width, pieces in win[rank]:
-        g.remote_dma_fused([transfer(cores[e], k, 1, S.xin, T.xq[:, a:a + width].bitcast(dt.uint8),
-                                     T.bq[:, b:b + width].bitcast(dt.uint8)) for e, a, b, k in pieces], local_sem=S.sent)
-    for width, pieces in win[rank]:
-        g.remote_dma_fused([transfer(cores[e], k, 1, S.xin, T.xs[:, a:a + width], T.bs[:, b:b + width])
-                            for e, a, b, k in pieces], local_sem=S.sent)
+    sent = [0, 0]
+    for i, step in enumerate(outward[rank]):
+        half = 0 if 2 * i < len(outward[rank]) else 1
+        local = (S.sent1, S.sent2)[half]
+        for w, ds in step:
+            sent[half] += send(ds, S.xin, local, lambda e: (T.xq[:, off[rank][e]:off[rank][e] + w].bitcast(dt.uint8),
+                                                            T.bq[:, slot[e][rank]:slot[e][rank] + w].bitcast(dt.uint8)))
+        for w, ds in step:
+            sent[half] += send(ds, S.xin, local, lambda e: (T.xs[:, off[rank][e]:off[rank][e] + w],
+                                                            T.bs[:, slot[e][rank]:slot[e][rank] + w]))
 
-    def hidden(wq, ws, rq, rs, m, zsem, tile, act):
-        for b in range(G):
-            g.tensor.matmul_mx(T.zp[:, 512 * b:512 * b + m], wq[:, 128 * b:128 * b + 128], ws[:, 128 * b:128 * b + 128],
-                               rq[:, 0:m], rs[:, 0:m], True, True).then_inc(S[zsem + str(b)], 1)
-        for b in (0, 2):
-            g.scalar.wait_ge(S[zsem + str(b)], 1)
-            g.scalar.activation(tile[:, b:4 * m:4], T.zp[:, 512 * b:512 * b + m], relu, scale=C).then_inc(act, 1)
-        for b in (1, 3):
-            v.wait_ge(S[zsem + str(b)], 1)
-            v.tensor_scalar(tile[:, b:4 * m:4], T.zp[:, 512 * b:512 * b + m], 0.0, C, mx, mul).then_inc(act, 1)
-        v.wait_ge(act, 4)
+    g.sync.dma_start(T.xb[:], T.x[:]).then_inc(S.ldx, 16)
+    g.sync.dma_start(T.w1b[:], T.w1[:]).then_inc(S.ldw, 16)
+    g.sync.dma_start(T.w2b[:], T.w2[:]).then_inc(S.ldw, 16)
+    g.sync.wait_ge(S.sent1, sent[0])
+    g.sync.dma_start(T.s1b[:], T.s1[:]).then_inc(S.lds1, 16)
+    g.sync.dma_start(T.s2b[:], T.s2[:]).then_inc(S.lds2, 16)
+    g.sync.wait_ge(S.ydone, 1)
+    g.sync.dma_start(T.y[:], T.yb[:]).then_inc(S.stored, 16)
+    g.sync.wait_ge(S.stored, 16)
 
-    arrivals = sum(2 for j in range(N) for _, ps in win[j] for p in ps if p[0] == rank)
     g.tensor.wait_ge(S.wdone, G + 1)
-    g.tensor.wait_ge(S.xin, arrivals)
-    hidden(T.w1q, T.w1s, T.bq, T.bs, n, "z", T.hb, S.hact)
-    v.quantize_mx(T.hq[:, 0:n], T.hs[:, 0:n], T.hb[:, 0:4 * n]).then_inc(S.hdone, 1)
+    g.tensor.wait_ge(S.xin, 2 * sum(_engines_of(outward[j], rank) for j in range(N)))
+    for b in range(G):
+        g.tensor.matmul_mx(T.zp[:, 512 * b:512 * b + NC], T.w1q[:, 128 * b:128 * b + 128], T.w1s[:, 128 * b:128 * b + 128],
+                           T.bq[:], T.bs[:], True, True).then_inc(S["z%d" % b], 1)
+    for b in (0, 2):
+        g.scalar.wait_ge(S["z%d" % b], 1)
+        g.scalar.activation(T.hb[:, b:4 * NC:4], T.zp[:, 512 * b:512 * b + NC], relu, scale=C).then_inc(S.hact, 1)
+    for b in (1, 3):
+        v.wait_ge(S["z%d" % b], 1)
+        v.tensor_scalar(T.hb[:, b:4 * NC:4], T.zp[:, 512 * b:512 * b + NC], 0.0, C, mx, mul).then_inc(S.hact, 1)
+    v.wait_ge(S.hact, G)
+    v.quantize_mx(T.hq[:], T.hs[:], T.hb[:]).then_inc(S.hdone, 1)
     g.tensor.wait_ge(S.hdone, 1)
-    g.tensor.matmul_mx(T.pp[:, 0:n], T.w2q[:], T.w2s[:], T.hq[:, 0:n], T.hs[:, 0:n], True, True).then_inc(S.pmm, 1)
+    g.tensor.matmul_mx(T.pp[:, 0:NC], T.w2q[:], T.w2s[:], T.hq[:], T.hs[:], True, True).then_inc(S.pmm, 1)
+    first = sum(w * len(ds) for w, ds in homeward[rank][0])
     v.wait_ge(S.pmm, 1)
-    v.tensor_copy(T.pb[:, 0:n], T.pp[:, 0:n]).then_inc(S.pcopy, 1)
+    v.tensor_copy(T.pb[:, 0:first], T.pp[:, 0:first]).then_inc(S.pcopy1, 1)
+    v.tensor_copy(T.pb[:, first:NC], T.pp[:, first:NC]).then_inc(S.pcopy2, 1)
 
-    g.wait_ge(S.pcopy, 1)
     left = 0
-    for w, js in _returns([(cnt[j][rank], j) for j in range(N) if cnt[j][rank]]):
-        k = ne // len(js)
-        g.remote_dma_fused([transfer(cores[j], k * i, k, S.back, T.pb[:, slot[rank][j]:slot[rank][j] + w],
-                                     T.land[:, off[j][rank]:off[j][rank] + w]) for i, j in enumerate(js)],
-                           local_sem=S.returned)
-        left += k * len(js)
+    for i, step in enumerate(homeward[rank]):
+        if i < 2:
+            g.wait_ge((S.pcopy1, S.pcopy2)[i], 1)
+        for w, ds in step:
+            left += send(ds, S.back, S.returned, lambda j: (T.pb[:, slot[rank][j]:slot[rank][j] + w],
+                                                            T.land[:, off[j][rank]:off[j][rank] + w]))
+    g.wait_ge(S.sent2, sent[1])
     g.wait_ge(S.returned, left)
 
-    v.wait_ge(S.lds, 32)
+    v.wait_ge(S.lds1, 16)
     for i in range(G):
         v.quantize_mx(T.s1q[:, 128 * i:128 * i + 128], T.s1s[:, 128 * i:128 * i + 128],
-                      T.s1b[:, 512 * i:512 * i + 512]).then_inc(S.sdone, 1)
-    v.quantize_mx(T.s2q[:], T.s2s[:], T.s2b[:]).then_inc(S.sdone, 1)
+                      T.s1b[:, 512 * i:512 * i + 512]).then_inc(S["s%d" % i], 1)
+    v.wait_ge(S.lds2, 16)
+    v.quantize_mx(T.s2q[:], T.s2s[:], T.s2b[:]).then_inc(S.s4, 1)
     g.tensor.wait_ge(S.xdone, 1)
-    g.tensor.wait_ge(S.sdone, G + 1)
-    hidden(T.s1q, T.s1s, T.xq, T.xs, NC, "y", T.kb, S.kact)
+    for b in range(G):
+        g.tensor.wait_ge(S["s%d" % b], 1)
+        g.tensor.matmul_mx(T.zp[:, 512 * b:512 * b + NC], T.s1q[:, 128 * b:128 * b + 128], T.s1s[:, 128 * b:128 * b + 128],
+                           T.xq[:], T.xs[:], True, True).then_inc(S["y%d" % b], 1)
+        g.scalar.wait_ge(S["y%d" % b], 1)
+        g.scalar.activation(T.kb[:, b:4 * NC:4], T.zp[:, 512 * b:512 * b + NC], relu, scale=C).then_inc(S.kact, 1)
+    v.wait_ge(S.kact, G)
     v.quantize_mx(T.kq[:], T.ks[:], T.kb[:]).then_inc(S.kdone, 1)
+    g.tensor.wait_ge(S.s4, 1)
     g.tensor.wait_ge(S.kdone, 1)
     g.tensor.matmul_mx(T.up[:, 0:NC], T.s2q[:], T.s2s[:], T.kq[:], T.ks[:], True, True).then_inc(S.umm, 1)
 
-    inc = 0
-    for e in range(N):
-        if cnt[rank][e]:
-            for w, js in _returns([(cnt[j][e], j) for j in range(N) if cnt[j][e]]):
-                if rank in js:
-                    inc += ne // len(js)
     v.wait_ge(S.umm, 1)
-    v.wait_ge(S.back, inc)
+    v.wait_ge(S.back, sum(_engines_of(homeward[e], rank) for e in range(N)))
     v.tensor_tensor(T.yb[:], T.up[:, 0:NC], T.land[:], add).then_inc(S.ydone, 1)

from concourse.bass import DstId, RemoteDMATransfer
from concourse.mybir import dt, AluOpType, ActivationFunctionType

N, NC, G, C = 10, 128, 4, 0.023

SEND = [(2, [1, 9, 3, 4, 5, 2, 6]), (2, [3, 4, 5, 7, 8, 9]), (2, [8, 4, 9, 3, 6, 7]), (2, [9, 7, 1, 6, 5, 4, 0]),
        (4, [9, 5, 7, 0, 3, 1]), (2, [3, 6, 7, 8, 1, 9, 2]), (2, [8, 3, 4, 2, 1, 9, 5]), (4, [3, 2, 1, 5, 0, 4]),
        (2, [9, 1, 0, 2, 3, 4, 6]), (2, [0, 7, 6, 8, 2, 1])]
BACK = [(2, [7, 3, 9, 4, 8]), (2, [3, 8, 5, 0, 4, 7, 9, 6]), (2, [8, 9, 7, 0, 5, 6]), (2, [4, 6, 2, 7, 0, 5, 1, 8]),
        (2, [0, 2, 3, 7, 8, 1, 6]), (2, [6, 3, 0, 7, 1, 4]), (2, [2, 0, 5, 9, 3, 8]), (2, [5, 1, 4, 2, 9, 3]),
        (4, [2, 1, 6, 5, 9]), (2, [6, 4, 1, 8, 0, 2, 5, 3])]

SCRATCH = {
    "xb": ("sbuf", [128, 4 * NC], "bfloat16"),
    "w1b": ("sbuf", [128, G * 512], "bfloat16"),
    "w2b": ("sbuf", [128, 512], "bfloat16"),
    "s1b": ("sbuf", [128, G * 512], "bfloat16"),
    "s2b": ("sbuf", [128, 512], "bfloat16"),
    "xq": ("sbuf", [128, NC], "float8_e4m3fn_x4"), "xs": ("sbuf", [128, NC], "uint8"),
    "w1q": ("sbuf", [128, G * 128], "float8_e4m3fn_x4"), "w1s": ("sbuf", [128, G * 128], "uint8"),
    "w2q": ("sbuf", [128, 128], "float8_e4m3fn_x4"), "w2s": ("sbuf", [128, 128], "uint8"),
    "s1q": ("sbuf", [128, G * 128], "float8_e4m3fn_x4"), "s1s": ("sbuf", [128, G * 128], "uint8"),
    "s2q": ("sbuf", [128, 128], "float8_e4m3fn_x4"), "s2s": ("sbuf", [128, 128], "uint8"),
    "bq": ("sbuf", [128, NC], "float8_e4m3fn_x4"), "bs": ("sbuf", [128, NC], "uint8"),
    "hb": ("sbuf", [128, 4 * NC], "bfloat16"),
    "hq": ("sbuf", [128, NC], "float8_e4m3fn_x4"), "hs": ("sbuf", [128, NC], "uint8"),
    "kb": ("sbuf", [128, 4 * NC], "bfloat16"),
    "kq": ("sbuf", [128, NC], "float8_e4m3fn_x4"), "ks": ("sbuf", [128, NC], "uint8"),
    "pb": ("sbuf", [128, NC], "float32"),
    "land": ("sbuf", [128, NC], "float32"),
    "yb": ("sbuf", [128, NC], "float32"),
    "zp": ("psum", [128, 512 * G], "float32"),
    "pp": ("psum", [128, 512], "float32"),
    "up": ("psum", [128, 512], "float32"),
}
SEMAPHORES = ["ldx", "ldw", "lds1", "lds2", "xdone", "wdone", "sent1", "sent2", "xin", "z0", "z1", "z2", "z3", "hact", "hdone",
              "pmm", "pcopy1", "pcopy2", "s0", "s1", "s2", "s3", "s4", "y0", "y1", "y2", "y3", "kact", "kdone", "umm", "back",
              "returned", "ydone", "stored"]


def _steps(plan, width, engines):
    lanes, order = plan
    out = []
    for s in range(0, len(order), lanes):
        js = order[s:s + lanes]
        k = engines // lanes
        while 2 * k * len(js) <= engines:
            k *= 2
        by = {}
        for i, j in enumerate(js):
            by.setdefault(width[j], []).append((j, k * i, k))
        out.append(list(by.items()))
    return out


def _engines_of(steps, rank):
    return sum(k for step in steps for _, ds in step for j, _, k in ds if j == rank)


def rank_program(g, core, T, topo):
    rank = T.rank_of(core)
    if rank is None:
        return
    cnt, cores = T.tables["CNT"], T.cores
    relu = ActivationFunctionType.Relu
    mx, mul, add = AluOpType.max, AluOpType.mult, AluOpType.add
    S, v = T.sem, g.vector

    off = [[sum(r[:e]) for e in range(N)] for r in cnt]
    slot = [{} for _ in range(N)]
    for e in range(N):
        a = 0
        for j in BACK[e][1]:
            slot[e][j] = a
            a += cnt[j][e]

    def engines(dst):
        m = topo.mask(core, dst)
        return [1 << i for i in range(m.bit_length()) if m >> i & 1]

    ne = min(len(engines(c)) for c in cores if c != core)
    outward = [_steps(SEND[j], cnt[j], ne) for j in range(N)]
    homeward = [_steps(BACK[e], [r[e] for r in cnt], ne) for e in range(N)]

    def send(ds, sem, local, piece):
        ts = []
        for j, first, k in ds:
            rid, pid, _ = topo.addr(cores[j])
            src, dst = piece(j)
            ts.append(RemoteDMATransfer(dst_ids=[DstId(rid=rid, pnc=pid)], remote_sem=sem, src=src, dst=dst,
                                        dma_engine_mask=sum(engines(cores[j])[first:first + k])))
        g.remote_dma_fused(ts, local_sem=local)
        return sum(k for _, _, k in ds)

    v.wait_ge(S.ldx, 16)
    v.quantize_mx(T.xq[:], T.xs[:], T.xb[:]).then_inc(S.xdone, 1)
    v.wait_ge(S.ldw, 32)
    for i in range(G):
        v.quantize_mx(T.w1q[:, 128 * i:128 * i + 128], T.w1s[:, 128 * i:128 * i + 128],
                      T.w1b[:, 512 * i:512 * i + 512]).then_inc(S.wdone, 1)
    v.quantize_mx(T.w2q[:], T.w2s[:], T.w2b[:]).then_inc(S.wdone, 1)

    g.wait_ge(S.xdone, 1)
    sent = [0, 0]
    for i, step in enumerate(outward[rank]):
        half = 0 if 2 * i < len(outward[rank]) else 1
        local = (S.sent1, S.sent2)[half]
        for w, ds in step:
            sent[half] += send(ds, S.xin, local, lambda e: (T.xq[:, off[rank][e]:off[rank][e] + w].bitcast(dt.uint8),
                                                            T.bq[:, slot[e][rank]:slot[e][rank] + w].bitcast(dt.uint8)))
        for w, ds in step:
            sent[half] += send(ds, S.xin, local, lambda e: (T.xs[:, off[rank][e]:off[rank][e] + w],
                                                            T.bs[:, slot[e][rank]:slot[e][rank] + w]))

    g.sync.dma_start(T.xb[:], T.x[:]).then_inc(S.ldx, 16)
    g.sync.dma_start(T.w1b[:], T.w1[:]).then_inc(S.ldw, 16)
    g.sync.dma_start(T.w2b[:], T.w2[:]).then_inc(S.ldw, 16)
    g.sync.wait_ge(S.sent1, sent[0])
    g.sync.dma_start(T.s1b[:], T.s1[:]).then_inc(S.lds1, 16)
    g.sync.dma_start(T.s2b[:], T.s2[:]).then_inc(S.lds2, 16)
    g.sync.wait_ge(S.ydone, 1)
    g.sync.dma_start(T.y[:], T.yb[:]).then_inc(S.stored, 16)
    g.sync.wait_ge(S.stored, 16)

    g.tensor.wait_ge(S.wdone, G + 1)
    g.tensor.wait_ge(S.xin, 2 * sum(_engines_of(outward[j], rank) for j in range(N)))
    for b in range(G):
        g.tensor.matmul_mx(T.zp[:, 512 * b:512 * b + NC], T.w1q[:, 128 * b:128 * b + 128], T.w1s[:, 128 * b:128 * b + 128],
                           T.bq[:], T.bs[:], True, True).then_inc(S["z%d" % b], 1)
    for b in (0, 2):
        g.scalar.wait_ge(S["z%d" % b], 1)
        g.scalar.activation(T.hb[:, b:4 * NC:4], T.zp[:, 512 * b:512 * b + NC], relu, scale=C).then_inc(S.hact, 1)
    for b in (1, 3):
        v.wait_ge(S["z%d" % b], 1)
        v.tensor_scalar(T.hb[:, b:4 * NC:4], T.zp[:, 512 * b:512 * b + NC], 0.0, C, mx, mul).then_inc(S.hact, 1)
    v.wait_ge(S.hact, G)
    v.quantize_mx(T.hq[:], T.hs[:], T.hb[:]).then_inc(S.hdone, 1)
    g.tensor.wait_ge(S.hdone, 1)
    g.tensor.matmul_mx(T.pp[:, 0:NC], T.w2q[:], T.w2s[:], T.hq[:], T.hs[:], True, True).then_inc(S.pmm, 1)
    first = sum(w * len(ds) for w, ds in homeward[rank][0])
    v.wait_ge(S.pmm, 1)
    v.tensor_copy(T.pb[:, 0:first], T.pp[:, 0:first]).then_inc(S.pcopy1, 1)
    v.tensor_copy(T.pb[:, first:NC], T.pp[:, first:NC]).then_inc(S.pcopy2, 1)

    left = 0
    for i, step in enumerate(homeward[rank]):
        if i < 2:
            g.wait_ge((S.pcopy1, S.pcopy2)[i], 1)
        for w, ds in step:
            left += send(ds, S.back, S.returned, lambda j: (T.pb[:, slot[rank][j]:slot[rank][j] + w],
                                                            T.land[:, off[j][rank]:off[j][rank] + w]))
    g.wait_ge(S.sent2, sent[1])
    g.wait_ge(S.returned, left)

    v.wait_ge(S.lds1, 16)
    for i in range(G):
        v.quantize_mx(T.s1q[:, 128 * i:128 * i + 128], T.s1s[:, 128 * i:128 * i + 128],
                      T.s1b[:, 512 * i:512 * i + 512]).then_inc(S["s%d" % i], 1)
    v.wait_ge(S.lds2, 16)
    v.quantize_mx(T.s2q[:], T.s2s[:], T.s2b[:]).then_inc(S.s4, 1)
    g.tensor.wait_ge(S.xdone, 1)
    for b in range(G):
        g.tensor.wait_ge(S["s%d" % b], 1)
        g.tensor.matmul_mx(T.zp[:, 512 * b:512 * b + NC], T.s1q[:, 128 * b:128 * b + 128], T.s1s[:, 128 * b:128 * b + 128],
                           T.xq[:], T.xs[:], True, True).then_inc(S["y%d" % b], 1)
        g.scalar.wait_ge(S["y%d" % b], 1)
        g.scalar.activation(T.kb[:, b:4 * NC:4], T.zp[:, 512 * b:512 * b + NC], relu, scale=C).then_inc(S.kact, 1)
    v.wait_ge(S.kact, G)
    v.quantize_mx(T.kq[:], T.ks[:], T.kb[:]).then_inc(S.kdone, 1)
    g.tensor.wait_ge(S.s4, 1)
    g.tensor.wait_ge(S.kdone, 1)
    g.tensor.matmul_mx(T.up[:, 0:NC], T.s2q[:], T.s2s[:], T.kq[:], T.ks[:], True, True).then_inc(S.umm, 1)

    v.wait_ge(S.umm, 1)
    v.wait_ge(S.back, sum(_engines_of(homeward[e], rank) for e in range(N)))
    v.tensor_tensor(T.yb[:], T.up[:, 0:NC], T.land[:], add).then_inc(S.ydone, 1)
